import numpy as np, ml_dtypes
CORES = [24,25,26,27,28,29,30,31]
N = 8
BF = ml_dtypes.bfloat16
def gentries(a):
    return np.ascontiguousarray(a.reshape(8, 16, -1).transpose(0, 2, 1)).reshape(8, -1)
def gtable(e):
    e = np.asarray(e); return np.ascontiguousarray(e.reshape(8, -1, 16).transpose(0, 2, 1)).reshape(128, -1).astype(np.int32)
W, R, PG, V, H = 2048, 32, 128, 6, 3
K = PG * R
def parts(rng):
    x = rng.integers(0, 256, (N, 8, 16, W)); e = rng.integers(0, 256, (N, 8, 16, PG)); w = rng.integers(0, 16, (N, 8, 16))
    h = rng.choice(np.array([1000, 1300, 1600, 1900]), (N, 8, 1)) + rng.integers(-300, 301, (N, 8, 16))
    l = rng.integers(0, W, (N, 8, K)); share = np.repeat(rng.choice(np.array([0.0, 0.3, 0.6, 0.9]), (N, 8, PG)), R, axis=2)
    s = np.where(rng.random((N, 8, K)) < share, l, rng.integers(0, W, (N, 8, K)))
    c = rng.random((N, 8, K)); p = np.where(c < 0.3, s, np.where(c < 0.4, l, rng.integers(0, W, (N, 8, K))))
    return x, e, w, h, p, s, l, rng.integers(0, W, (N, 8, K))
def pack(x, e, w, h, p, s, l, q):
    r = {"xt": x.reshape(N, 128, W).astype(np.float32).astype(BF), "ed": e.reshape(N, 128, PG).astype(np.float32).astype(BF),
         "wt": np.ascontiguousarray(w.reshape(N, 128, 1)).astype(np.int32), "th": np.ascontiguousarray(h.reshape(N, 128, 1)).astype(np.int32)}
    for k, z in (("pl", p), ("sl", s), ("ll", l), ("ql", q)): r[k] = np.stack([gtable(a) for a in z])
    return r
def setup_inputs(rng):
    return pack(*parts(rng))
def setup_inputs_spread(rng):
    x, e, w, h, p, s, l, q = parts(rng)
    x = np.minimum((np.exp2(8 * rng.random((N, 8, 1, W))) * rng.random((N, 8, 16, W))).astype(np.int64), 255)
    e = np.minimum((np.exp2(8 * rng.random((N, 8, 1, PG))) * rng.random((N, 8, 16, PG))).astype(np.int64), 255)
    w = (16 * rng.random((N, 8, 16)) ** 3).astype(np.int64); h = np.minimum(np.exp2(12 * rng.random((N, 8, 16))).astype(np.int64) - 1, 4080)
    p, s, l, q = [(W * rng.random((N, 8, K)) ** 3).astype(np.int64) for z in range(4)]
    s = np.where(rng.random((N, 8, K)) < np.repeat(rng.random((N, 8, PG)), R, axis=2), l, s)
    return pack(x, e, w, h, p, s, l, q)
def setup_inputs_ends(rng):
    x = 255 * rng.integers(0, 2, (N, 8, 16, W)); e = 255 * rng.integers(0, 2, (N, 8, 16, PG)); w = 15 * rng.integers(0, 2, (N, 8, 16)); h = 4080 * rng.integers(0, 2, (N, 8, 16))
    kind = rng.integers(0, 3, (N, 8, 1)); kind[:, 7] = 0; kind[0, 0] = 0; kind[1, 1] = 1
    x[..., 0] = np.where(kind == 0, 0, np.where(kind == 1, 255, x[..., 0])); x[..., W - 1] = np.where(kind == 0, 255, np.where(kind == 1, 0, x[..., W - 1]))
    w[:, :, 5] = 0; w[:, 7] = 15; w[:, :, 2] = 15; w[:, :, 13] = 15
    h[:, :, 0] = 0; h[:, :, 15] = 0; h[:, :, 1] = 4080; h[:, :, 14] = 4080
    p, s, l, q = [np.where(rng.random((N, 8, K)) < 0.75, (W - 1) * rng.integers(0, 2, (N, 8, K)), rng.integers(0, W, (N, 8, K))) for z in range(4)]
    pv, sv, lv = [z.reshape(N, 8, PG, R) for z in (p, s, l)]; k = np.arange(R)
    for i in (0, 1, 2, 3, PG - 4, PG - 3, PG - 2, PG - 1):
        pv[:, :, i] = 0; sv[:, :, i] = W - 1; lv[:, :, i] = W - 1
    lv[:, :, [0, PG - 1]] = np.where(k % 4 == 1, 0, W - 1)
    lv[:, :, [1, PG - 2]] = np.where((k % 4 == 1) | (k == 2), 0, W - 1)
    lv[:, :, [3, PG - 4]] = 0
    e[..., [0, PG - 1]] = 0; e[:, :, 2, [0, PG - 1]] = 255; e[:, :, 13, [0, PG - 1]] = 18
    e[..., [2, PG - 3]] = 0; e[..., [3, PG - 4]] = 255
    return pack(x, e, w, h, p, s, l, q)
def setup_inputs_corners(rng):
    x, e, w, h, p, s, l, q = parts(rng)
    cnt = np.roll(np.array([31, 32, 0, 8 * PG, 33, 1, 8 * PG - 1, 64])[:N], int(rng.integers(0, N))); fl = np.zeros((N, 8 * PG), bool)
    for r in range(N): fl[r, rng.permutation(8 * PG)[:int(cnt[r])]] = True
    fr = np.repeat(fl.reshape(N, 8, PG), R, axis=2)
    lv = l.reshape(N, 8, PG, R); lv[:, :, [0, PG - 1]] = (W - 1) * rng.integers(0, 2, (N, 8, 2, R))
    far = (l + rng.integers(1, W, l.shape)) % W; half = np.repeat(rng.random((N, 8, PG)) < 0.5, R, axis=2)
    s = np.where(fr, far, l); p = np.where(fr | half, l, rng.integers(0, W, l.shape))
    for g in range(8):
        if g % 4 < 3: q[:, g] = (l, s, p)[g % 4][:, g]
    w[:, 0] = 0; w[:, 7] = 15; w[:, 4] = 15; w[:, 3] = 0; w[:, 3, 15] = 15; w[:, 5] = 0; w[:, 5, 0] = 1
    h = np.where(rng.random(h.shape) < 0.5, rng.choice(np.array([0, 1, 4079, 4080]), h.shape), h)
    e[..., [0, PG - 1]] = 0; e[:, :, 2, [0, PG - 1]] = 255; e[:, :, 13, [0, PG - 1]] = 18
    e[..., 1] = 255; e[..., PG - 2] = 0
    return pack(x, e, w, h, p, s, l, q)
def setup_inputs_alike(rng):
    x, e, w, h, p, s, l, q = parts(rng)
    step = rng.choice(np.array([1, 4, 8, 32]), (N, 8, 1, 1)); lane = rng.integers(0, 8, (N, 8, 16, 1))
    x = step * (rng.integers(0, 8, (N, 8, 1, W)) ^ lane); e = step * (rng.integers(0, 8, (N, 8, 1, PG)) ^ lane)
    h = step[..., 0] * rng.integers(20, 81, (N, 8, 16))
    return pack(x, e, w, h, p, s, l, q)
def setup_inputs_near(rng):
    x, e, w, h, p, s, l, q = parts(rng); n = np.arange(N); f = rng.integers(0, 16, N); k = np.arange(R)
    s[:, 0] = l[:, 0]; h[:, 0] = 0
    h[:, 7] = 4080; x[:, 7, :, :2] = 0; x[:, 7, :, W - 2:] = 255; x[n, 7, f, 1] = 1; x[n, 7, f, W - 2] = 254
    pv, sv, lv, qv = [z.reshape(N, 8, PG, R)[:, 7] for z in (p, s, l, q)]
    for z in (pv, sv, lv): z[:, PG - 1] = W - 1; z[:, PG - 3] = W - 1
    pv[:, PG - 1, R - 4:] = 0; sv[:, PG - 1, R - 4:] = 0; qv[:, PG - 1, R - 4:] = W - 2
    pv[:, PG - 2] = 0; sv[:, PG - 2] = W - 1; sv[:, PG - 2, 0] = W - 2; lv[:, PG - 2] = np.where(k % 4 == 1, 0, W - 1)
    e[:, 7, :, PG - 3] = 0; e[n, 7, f, PG - 3] = 1
    pv[:, PG - 4] = 1; sv[:, PG - 4] = 0; lv[:, PG - 4] = W - 1
    return pack(x, e, w, h, p, s, l, q)
def check_inputs(d):
    bad = []
    for k, hi in (("xt", 255), ("ed", 255), ("wt", 15), ("th", 4080), ("pl", W - 1), ("sl", W - 1), ("ll", W - 1), ("ql", W - 1)):
        v = np.asarray(d[k]).astype(np.float64)
        if not (np.min(v) >= 0 and np.max(v) <= hi): bad.append("range of " + k)
        elif np.any(v != np.floor(v)): bad.append("whole numbers of " + k)
    return bad
def dist(y, z):
    return np.add.reduce(np.abs(y - z), axis=1, dtype=np.int32)
def reference(xt, ed, wt, th, pl, sl, ll, ql):
    x = xt.astype(np.float32).astype(np.int16).reshape(N, 8, 16, W); e = ed.astype(np.float32).astype(np.int16).reshape(N, 8, 16, PG)
    w = wt.astype(np.int32).reshape(N, 8, 16, 1); h = th.astype(np.int32).reshape(N, 8, 16)[:, :, np.arange(K) % 16]
    p, s, l, q = [np.stack([gentries(a) for a in z]).astype(np.int64) for z in (pl, sl, ll, ql)]
    more = 37 * (np.arange(K) % R); A = np.zeros(N, np.int64)
    for t in range(V):
        new = np.zeros_like(l); failed = np.zeros((N, 8, PG), bool); m = np.zeros((N, 8, 16, PG), np.int16)
        for r in range(N):
            vp, vs, vl, vq = [np.take_along_axis(x[r], z[r][:, None, :], 2) for z in (p, s, l, q)]
            a = dist(vp, vs); b = dist(vs, vl); c = dist(vp, vl); d = dist(vq, vs); o = dist(vl, np.repeat(e[r], R, axis=2))
            failed[r] = 2 * np.sum((c - b).reshape(8, PG, R), axis=2) < np.sum(a.reshape(8, PG, R), axis=2)
            u = np.repeat(np.sum(w[r] * e[r], axis=1) & (W - 1), R, axis=1).astype(np.int64)
            change = ((l[r] * u >> 5) + l[r] + more + A[r]) & (W - 1)
            new[r] = np.where(np.repeat(failed[r], R, axis=1) & (c < b), p[r], np.where(d < b, q[r], np.where(o >= h[r], change, l[r])))
            m[r] = np.max(vl.reshape(8, 16, PG, R), axis=3)
        got = np.roll(m, N // 2, axis=0)
        e = np.where(failed[:, :, None, :], np.abs(e - got), (e + got) >> 1)
        A = np.sum(failed, axis=(1, 2)).astype(np.int64) & 31
        q = np.where(new != l, l, q); p, s, l = s, l, new
        if t < V - 1: p, s, l, q = [np.roll(z, H, axis=0) for z in (p, s, l, q)]
    out = [np.stack([gtable(a) for a in z]).astype(np.float32) for z in (p, s, l, q)]
    return {"yp": out[0], "ys": out[1], "yl": out[2], "yq": out[3], "ye": e.reshape(N, 128, PG).astype(np.float32).astype(BF)}

import numpy as np
from concourse.mybir import AluOpType as OP, ActivationFunctionType as AF, AxisListType

NV, HOP, NC = 6, 3, 8
W = 2048
WX = W + 384
CH = 2048
BIG = 8192.0
DABS = {(t, 0) for t in range(5)}
ASTAT, BSPLIT = True, True
FIRST = {"s": -5.0, "l": -5.0, "dq": 5.0, "rq": -10.0, "vb": -5.0, "vc": -5.0, "vo": -10.0, "R": -10.0, "SB": -5.0, "MB": -5.0}

FT = {}
IT = {}


def _fields(d, items):
    o = 0
    for k, n in items:
        d[k] = (o, n)
        o += n
    return o


NF = _fields(FT, [("LU", 128), ("CHp", 128), ("r3", 128), ("r2", 128), ("w", 64), ("PF", 128), ("LQ", 128),
                  ("Csb", 128), ("Bsb", 128), ("As1", 8), ("As2", 64), ("junk", 64), ("cnt", 8)])
NI = _fields(IT, [("ui", 64), ("ua", 64), ("LUi", 128), ("CHi", 128), ("r1", 128), ("h", 64)])

SCRATCH = {
    "tp": ("sbuf", [128, 256], "int32"), "tsx": ("sbuf", [128, 256], "int32"),
    "tl": ("sbuf", [128, 256], "int32"), "tq": ("sbuf", [128, 256], "int32"),
    "Lnum": ("sbuf", [128, 6 * 256], "int32"), "Loff": ("sbuf", [128, 9 * 256], "uint16"),
    "Qoff": ("sbuf", [128, 6 * 256], "uint16"), "Qv": ("sbuf", [128, 6 * 256], "float32"),
    "L6": ("sbuf", [128, 6 * 256], "float32"),
    "finPS": ("sbuf", [128, 512], "float32"), "finLQ": ("sbuf", [128, 512], "float32"),
    "fPS": ("sbuf", [128, 512], "float32"), "fLQ": ("sbuf", [128, 512], "float32"),
    "tf": ("sbuf", [128, 4 * NF], "float32"), "ti": ("sbuf", [128, 4 * NI], "int32"),
    "E0": ("sbuf", [128, 128], "bfloat16"),
    "mmsg": ("sbuf", [128, 12 * 64], "bfloat16"), "mland": ("sbuf", [128, 12 * 64], "bfloat16"),
    "emsg": ("sbuf", [128, 12 * 80], "bfloat16"), "eland": ("sbuf", [128, 12 * 80], "bfloat16"),
    "idf": ("sbuf", [128, 128], "float32"), "grp8": ("sbuf", [128, 128], "float32"), "pair": ("sbuf", [128, 64], "float32"),
    "pr0": ("sbuf", [128, 64], "bfloat16"), "pr1": ("sbuf", [128, 64], "bfloat16"),
    "gr0": ("sbuf", [128, 128], "bfloat16"), "gr1": ("sbuf", [128, 128], "bfloat16"),
    "ETs": ("sbuf", [128, 4 * 128], "bfloat16"),
    "Ind": ("sbuf", [128, 2048], "bfloat16"), "maskz": ("sbuf", [128, 2048], "bfloat16"),
    "one": ("sbuf", [128, 2048], "bfloat16"), "idn": ("sbuf", [128, 128], "bfloat16"),
    "nidn": ("sbuf", [128, 128], "bfloat16"), "blk0": ("sbuf", [128, 128], "bfloat16"),
    "blk": ("sbuf", [128, 128], "bfloat16"), "blkP": ("sbuf", [128, 128], "bfloat16"),
    "blkN": ("sbuf", [128, 128], "bfloat16"), "blk2": ("sbuf", [128, 128], "float32"),
    "Bp": ("sbuf", [128, 144], "bfloat16"), "Bn": ("sbuf", [128, 144], "bfloat16"),
    "o16": ("sbuf", [128, 128], "bfloat16"),
    "kin": ("sbuf", [128, 16], "int32"), "k37": ("sbuf", [128, 8], "float32"),
    "wti": ("sbuf", [128, 8], "int32"), "thi": ("sbuf", [128, 8], "int32"),
    "tci": ("sbuf", [128, 16], "int32"), "tcf": ("sbuf", [128, 16], "float32"),
    "ai": ("sbuf", [128, 6 * 16], "int32"), "af": ("sbuf", [128, 6 * 16], "float32"),
    "R0": ("psum", [128, 1024], "float32"), "R1": ("psum", [128, 1024], "float32"),
    "SB": ("psum", [128, 512], "float32"), "CB": ("psum", [128, 512], "float32"),
    "ZB": ("psum", [128, 512], "float32"), "MB": ("psum", [128, 512], "float32"),
}
for _t in range(NV):
    SCRATCH["win%d" % _t] = ("sbuf", [128, WX], "bfloat16")
for _z in range(4):
    for _n in ("s", "dp", "ra"):
        SCRATCH["%s%d" % (_n, _z)] = ("sbuf", [128, CH], "bfloat16")
for _z in range(2):
    for _n in ("l", "dq", "rq", "vb", "vc", "vo", "sc"):
        SCRATCH["%s%d" % (_n, _z)] = ("sbuf", [128, CH], "bfloat16")

SEMAPHORES = (["sV", "sS", "sP", "sG", "lsem", "fa", "fb", "fc"] + ["w%d" % t for t in range(1, NV)]
              + ["m%d" % i for i in range(12)] + ["e%d" % i for i in range(12)]
              + ["ld%d" % i for i in range(9)] + ["st%d" % i for i in range(10)])

CYC = 0.83e-3 * 1.2
PEC = 0.417e-3 * 1.2
GAM = 1.5


def rank_program(g, core, T, topo):
    rank = T.rank_of(core)
    if rank is None:
        return
    ENG = {"V": g.vector, "S": g.scalar, "P": g.tensor, "G": g, "Y": g.sync}
    ESEM = {"V": "sV", "S": "sS", "P": "sP", "G": "sG"}
    PSUM = ("R0", "R1", "SB", "CB", "ZB", "MB")
    ops = []
    acc = {}
    boost = [1000.0]

    def R(b, lo, hi, st=1, p=None):
        return (b, lo, hi, st, p)

    def ap(r):
        b, lo, hi, st, p = r
        sl = slice(lo, hi, st) if st != 1 else slice(lo, hi)
        return T[b][p[0]:p[1], sl] if p else T[b][:, sl]

    def n_of(r):
        return (r[2] - r[1] + r[3] - 1) // r[3]

    def ps(r):
        return r[0] in PSUM

    def overlap(a, b):
        if a[1] >= b[2] or b[1] >= a[2]:
            return False
        if a[3] == b[3] and a[3] > 1 and (a[1] - b[1]) % a[3] != 0:
            return False
        return True

    def op(eng, emit, rd, wr, occ, lat=None, sem=None, inc=0, deps=()):
        k = len(ops)
        dep = set(deps)
        for w, regs in ((False, rd), (True, wr)):
            for r in regs:
                lst = acc.setdefault(r[0], [])
                psb = r[0] in PSUM
                for (k2, r2, w2) in lst:
                    if k2 == k:
                        continue
                    if psb and ops[k2]["eng"] != eng:
                        if r[1] // 512 <= (r2[2] - 1) // 512 and r2[1] // 512 <= (r[2] - 1) // 512:
                            dep.add(k2)
                            continue
                    if (w or w2) and overlap(r, r2):
                        dep.add(k2)
        for w, regs in ((False, rd), (True, wr)):
            for r in regs:
                lst = acc[r[0]]
                if w and r[3] == 1 and r[0] not in PSUM:
                    lst[:] = [x for x in lst if x[0] == k or not (x[1][1] >= r[1] and x[1][2] <= r[2])]
                lst.append((k, r, w))
        ops.append({"eng": eng, "emit": emit, "dep": dep, "occ": occ, "lat": occ + 0.03 if lat is None else lat,
                    "sem": sem, "inc": inc, "boost": boost[0] + FIRST.get((wr[0][0] if wr else "-").rstrip("0123456789"), 0.0)})
        return k

    def vcost(n, f=1.0):
        return 0.06 + max(64, n * f) * CYC

    def two(*rs):
        for r in rs:
            if not (r[0] in SCRATCH and SCRATCH[r[0]][2] in ("bfloat16", "uint16", "float16")) or ps(r):
                return 1.0
        return 0.5

    def vtt(out, a, b, alu):
        f = 1.0 if (ps(a) or ps(b)) else 2.0
        return op("V", lambda e: [e.tensor_tensor(out=ap(out), in0=ap(a), in1=ap(b), op=alu)], [a, b], [out], vcost(n_of(out), f))

    def vts(out, a, s1, op0, s2=None, op1=None):
        cols = [x for x in (s1, s2) if isinstance(x, tuple)]

        def em(e):
            x1 = ap(s1) if isinstance(s1, tuple) else s1
            x2 = ap(s2) if isinstance(s2, tuple) else s2
            if op1 is None:
                return [e.tensor_scalar(out=ap(out), in0=ap(a), scalar1=x1, scalar2=None, op0=op0)]
            return [e.tensor_scalar(out=ap(out), in0=ap(a), scalar1=x1, scalar2=x2, op0=op0, op1=op1)]
        return op("V", em, [a] + cols, [out], vcost(n_of(out), two(out, a)))

    def vcopy(out, a):
        return op("V", lambda e: [e.tensor_copy(out=ap(out), in_=ap(a))], [a], [out], vcost(n_of(out), two(out, a)))

    def vset(out, c):
        return op("V", lambda e: [e.memset(ap(out), c)], [], [out], vcost(n_of(out), two(out)))

    def act(out, a, func, scale=1.0, acc_out=None):
        def em(e):
            if acc_out is not None:
                return [e.activation(out=ap(out), in_=ap(a), func=func, accum_out=ap(acc_out))]
            return [e.activation(out=ap(out), in_=ap(a), func=func)]
        return op("S", em, [a], [out] + ([acc_out] if acc_out else []), 0.08 + max(64, n_of(out)) * CYC)

    def gath_s(out, win, off):
        return op("S", lambda e: [e.activation(out=ap(out), in_=ap(win).indirect(ap(off)), func=AF.Copy)], [win, off], [out],
                  0.08 + n_of(out) * GAM * CYC)

    def gath_sub(out, win, off, b):
        return op("V", lambda e: [e.tensor_tensor(out=ap(out), in0=ap(win).indirect(ap(off)), in1=ap(b), op=OP.subtract)],
                  [win, off, b], [out], 0.06 + n_of(out) * GAM * CYC)

    def pe(mms):
        rd, wr, cost = [], [], 0.0
        for (o, l, r, a, z) in mms:
            for x in (l, r):
                if x not in rd:
                    rd.append(x)
            if o not in wr:
                wr.append(o)
            f = 4.0 if SCRATCH[r[0]][2] == "float32" else 1.0
            cost += f * max(min(64, n_of(l)), n_of(r)) * PEC

        def em(e):
            return [e.matmul(out=ap(o), lhsT=ap(l), rhs=ap(r), start=a, stop=z) for (o, l, r, a, z) in mms]
        rd2 = {}
        for x in rd:
            key = x[0]
            if key in rd2:
                rd2[key] = (key, min(rd2[key][1], x[1]), max(rd2[key][2], x[2]), 1, None)
            else:
                rd2[key] = x
        return op("P", em, list(rd2.values()), wr, cost + 0.03, cost + 0.1)

    def gsel(out, a, pattern, cmp, base, cm):
        return op("G", lambda e: [e.affine_select(out=ap(out), in_=ap(a), pattern=pattern, compare_op=cmp, fill=0.0, base=base,
                                                  channel_multiplier=cm)], [a], [out], 0.2 + 2 * n_of(out) * CYC)

    def load(q, out, name, sem):
        occ = 0.1
        return op(q, lambda e: [e.dma_start(out=ap(out), in_=T[name][:])], [], [out], occ, 3.0, sem=sem, inc=16)

    def store(q, name, lo, hi, src, sem):
        return op(q, lambda e: [e.dma_start(out=T[name][:, lo:hi], in_=ap(src))], [src], [("out_" + name, lo, hi, 1, None)], 0.1, 3.0,
                  sem=sem, inc=16)

    nsent = [0]

    def send(dst_rank, out, src, sem, lat=2.5, occ=0.8):
        dst = T.cores[dst_rank % NC]
        rid, pid = topo.addr(dst)[0], topo.addr(dst)[1]
        mask = topo.mask(core, dst)
        n = len(topo.engines(core, dst))
        nsent[0] += n
        k = op("G", lambda e: [e.remote_dma(ap(out), ap(src), T.sem[sem], T.sem.lsem, pid, rid, mask)], [src], [], occ, occ,
               sem="lsem", inc=0)
        return op("N", None, [], [out], 0.0, lat, sem=sem, inc=n, deps=(k,))

    def send_columns(t):
        send(rank - HOP * t, R("win%d" % t, 0, WX), R("win0", 0, WX), "w%d" % t, 7.0)

    I, NIDN, ONE, BLK = R("idn", 0, 128), R("nidn", 0, 128), R("one", 0, 128), R("blk", 0, 128)
    load("Y", R("win0", 0, W), "xt", "ld0")
    load("S", R("tsx", 0, 256), "sl", "ld1")
    load("S", R("tp", 0, 256), "pl", "ld2")
    load("Y", R("wti", 0, 1), "wt", "ld3")
    load("Y", R("thi", 0, 1), "th", "ld4")
    load("S", R("tl", 0, 256), "ll", "ld5")
    load("S", R("tq", 0, 256), "ql", "ld6")
    load("Y", R("E0", 0, 128), "ed", "ld7")
    vset(R("one", 0, 128), 1.0)
    gsel(I, ONE, [[-1, 128]], OP.is_equal, 0, 1)
    gsel(R("blk0", 0, 128), ONE, [[-16, 8], [0, 16]], OP.is_ge, 0, 1)
    gsel(BLK, R("blk0", 0, 128), [[16, 8], [0, 16]], OP.is_ge, 15, -1)
    vcopy(R("tcf", 0, 1), R("wti", 0, 1))
    vts(R("tci", 0, 1), R("thi", 0, 1), -1, OP.add)
    vts(R("tci", 4, 5), R("tci", 0, 1), 4, OP.arith_shift_right)
    vts(R("tci", 8, 9), R("tci", 0, 1), 15, OP.bitwise_and)
    vcopy(R("tcf", 4, 5), R("tci", 4, 5))
    vcopy(R("tcf", 8, 9), R("tci", 8, 9))
    vts(R("win0", W, W + 128), BLK, R("tcf", 0, 1), OP.mult)
    vts(R("win0", W + 128, W + 256), I, R("tcf", 4, 5), OP.mult, -16.0 * BIG, OP.mult)
    vts(R("win0", W + 256, W + 384), I, R("tcf", 8, 9), OP.mult, -BIG, OP.mult)
    send_columns(1)
    boost[0] = 0.0
    vset(R("one", 128, 2048), 1.0)
    op("G", lambda e: [e.iota(ap(R("kin", 0, 1)), [[0, 1]], 0, 1)], [], [R("kin", 0, 1)], 0.2)
    gsel(R("Ind", 0, 2048, 1, (0, 64)), R("one", 0, 2048, 1, (0, 64)), [[-1, 64], [0, 32]], OP.is_equal, 0, 1)
    if ASTAT:
        P8 = (0, 8)
        gsel(R("pr0", 0, 64), R("one", 0, 64), [[-2, 64]], OP.is_ge, 0, 1)
        gsel(R("pr1", 0, 64), R("pr0", 0, 64), [[2, 64]], OP.is_ge, 1, -1)
        vcopy(R("pair", 0, 64), R("pr1", 0, 64))
        gsel(R("gr0", 0, 128, 1, P8), R("one", 0, 128, 1, P8), [[1, 128]], OP.is_ge, 0, -16)
        gsel(R("gr1", 0, 128, 1, P8), R("gr0", 0, 128, 1, P8), [[-1, 128]], OP.is_ge, 15, 16)
        vcopy(R("grp8", 0, 128, 1, P8), R("gr1", 0, 128, 1, P8))
    if BSPLIT:
        vcopy(R("idf", 0, 128), I)
    vts(NIDN, I, -1.0, OP.mult)
    vset(R("Bp", 0, 144), 0.0)
    vset(R("Bn", 0, 144), 0.0)
    vts(R("Bp", 15, 128, 16), R("blk", 0, 128, 16), BIG, OP.mult)
    vts(R("Bn", 15, 128, 16), R("blk", 0, 128, 16), -BIG, OP.mult)
    vts(R("blkP", 0, 128), BLK, BIG, OP.mult)
    vts(R("blkN", 0, 128), BLK, -BIG, OP.mult)
    vts(R("blk2", 0, 128), BLK, 2.0, OP.mult)
    vset(R("o16", 0, 128), 0.0625)
    vset(R("maskz", 0, CH), 1.0)
    vset(R("maskz", 0, CH, 32), 0.0)
    vset(R("emsg", 0, 12 * 80), 0.0)
    vts(R("kin", 8, 9), R("kin", 0, 1), 15, OP.bitwise_and)
    vts(R("k37", 0, 1), R("kin", 8, 9), 32.0 * 37.0, OP.mult)
    vts(R("k37", 1, 2), R("kin", 8, 9), 32.0 * 37.0, OP.mult, 32.0 * 37.0 * 16.0, OP.add)

    def Ln(k, X):
        if k <= 0:
            return R(("tp", "tsx", "tl")[k + 2], 128 * X, 128 * X + 128)
        return R("Lnum", (k - 1) * 256 + 128 * X, (k - 1) * 256 + 128 * X + 128)

    def Lu(k, X, h):
        o = (k + 2) * 256 + 128 * X
        return R("Loff", o, o + 128) if h is None else R("Loff", o + 64 * h, o + 64 * h + 64)

    def Qu(t, X, h):
        o = t * 256 + 128 * X
        return R("Qoff", o, o + 128) if h is None else R("Qoff", o + 64 * h, o + 64 * h + 64)

    def Qv(t, X):
        return R("Qv", t * 256 + 128 * X, t * 256 + 128 * X + 128)

    def L6(k, X):
        return R("L6", (k + 2) * 256 + 128 * X, (k + 2) * 256 + 128 * X + 128)

    def every(r, h):
        return R(r[0], r[1] + h, r[2], 2)

    for k, nm in ((-1, "tsx"), (-2, "tp"), (0, "tl")):
        vcopy(R("Loff", (k + 2) * 256, (k + 2) * 256 + 256), R(nm, 0, 256))
    vcopy(R("Qoff", 0, 256), R("tq", 0, 256))
    vts(R("Qv", 0, 256), R("tq", 0, 256), 4096.0, OP.add)
    for k, nm in ((-2, "tp"), (-1, "tsx"), (0, "tl")):
        vts(R("L6", (k + 2) * 256, (k + 2) * 256 + 256), R(nm, 0, 256), 6144.0, OP.add)

    def sums(out, parts, extra=()):
        mm = []
        for (coef, tile, base) in parts:
            for i in range(16):
                mm.append([out, R(coef, 15 - i, 143 - i), R(tile, base + i, base + 1024, 16)])
        for (lt, rh) in extra:
            mm.append([out, lt, rh])
        return [(o, l, r, j == 0, j == len(mm) - 1) for j, (o, l, r) in enumerate(mm)]

    for t in range(NV):
        wn = "win%d" % t
        WIN = R(wn, 0, W)
        for X in range(2):
            z, y, sl = (t % 2) * 2 + X, X, 2 * t + X

            def F(nm):
                o, n = FT[nm]
                return R("tf", z * NF + o, z * NF + o + n)

            def J(nm):
                o, n = IT[nm]
                return R("ti", z * NI + o, z * NI + o + n)

            def tile(nm, q, h=None):
                return R("%s%d" % (nm, q), 0, CH) if h is None else R("%s%d" % (nm, q), 1024 * h, 1024 * h + 1024)

            E = R("E0", 64 * X, 64 * X + 64) if t == 0 else R("eland", (sl - 2) * 80, (sl - 2) * 80 + 64)
            for h in range(2):
                gath_s(tile("s", z, h), WIN, Lu(t - 1, X, h))
            for h in range(2):
                gath_sub(tile("dp", z, h), WIN, Lu(t - 2, X, h), tile("s", z, h))
            vts(tile("ra", z), tile("dp", z), 0.0, OP.max, 2.0, OP.mult)
            if ASTAT:
                A1, A2 = R("ZB", 448, 456), R("ZB", 448, 512, 1, (0, 8))
                mm = []
                for k in range(16):
                    mm.append((A1, R("ra%d" % z, k, CH, 16), R("blkP", 0, 128, 16), k == 0, False))
                    mm.append((A1, R("dp%d" % z, k, CH, 16), R("blkN", 0, 128, 16), False, k == 15))
                pe(mm)
                act(F("As1"), A1, AF.Copy)
                pe([(A2, F("As1"), R("pair", 0, 64), True, True)])
                act(R(F("As2")[0], F("As2")[1], F("As2")[2], 1, (0, 8)), A2, AF.Copy)
            pe([(R("MB", 0, 128, 1, (0, 64)), E, NIDN, True, True), (R("MB", 128, 192), R(wn, W, W + 128), E, True, True)])
            ET = R("ETs", z * 128, z * 128 + 128, 1, (0, 64))
            act(ET, R("MB", 0, 128, 1, (0, 64)), AF.Copy)
            vcopy(J("ui"), R("MB", 128, 192))
            vts(J("ua"), J("ui"), 2047, OP.bitwise_and)
            U32, L4 = R("ZB", 128, 192), R("ZB", 192, 320)
            vts(U32, J("ua"), 32.0, OP.add)
            L = Ln(t, X)
            for h in range(2):
                vtt(every(F("LU"), h), every(L, h), U32, OP.mult)
            vts(L4, L, 4096.0, OP.add)
            vtt(F("LQ"), L4, Qv(t, X), OP.subtract)
            for h in range(2):
                gath_s(tile("l", y, h), WIN, Lu(t, X, h))
            for h in range(2):
                gath_sub(tile("dq", y, h), WIN, Qu(t, X, h), tile("s", z, h))
            if (t, X) in DABS:
                for h in range(2):
                    act(tile("rq", y, h), tile("dq", y, h), AF.Abs)
            else:
                vts(tile("rq", y), tile("dq", y), 0.0, OP.max, 2.0, OP.mult)
            op("V", lambda e, a=tile("sc", y), b=R("maskz", 0, CH), c=tile("l", y): [e.tensor_tensor_scan(
                out=ap(a), data0=ap(b), data1=ap(c), initial=0.0, op0=OP.mult, op1=OP.max)],
                [R("maskz", 0, CH), tile("l", y)], [tile("sc", y)], vcost(CH, 0.5))
            M = R("mmsg", sl * 64, sl * 64 + 64)
            act(M, R("sc%d" % y, 31, CH, 32), AF.Copy)
            MR = R("mland", sl * 64, sl * 64 + 64)
            send(rank + 4, MR, M, "m%d" % sl)
            if X == 1 and t + 2 < NV:
                send_columns(t + 2)
            for h in range(2):
                rb = "R%d" % h
                mm = []
                for j in range(2):
                    o, c0 = R(rb, 512 * j, 512 * j + 512), 1024 * h + 512 * j
                    mm.append((o, I, R("s%d" % z, c0, c0 + 512), True, False))
                    mm.append((o, NIDN, R("l%d" % y, c0, c0 + 512), False, True))
                pe(mm)
                act(tile("vb", y, h), R(rb, 0, 1024), AF.Abs)
            for h in range(2):
                rb = "R%d" % h
                mm = []
                for j in range(2):
                    o, c0 = R(rb, 512 * j, 512 * j + 512), 1024 * h + 512 * j
                    mm.append((o, I, R("s%d" % z, c0, c0 + 512), True, False))
                    mm.append((o, I, R("dp%d" % z, c0, c0 + 512), False, False))
                    mm.append((o, NIDN, R("l%d" % y, c0, c0 + 512), False, True))
                pe(mm)
                act(tile("vc", y, h), R(rb, 0, 1024), AF.Abs)
            for h in range(2):
                rb = "R%d" % h
                mm = []
                for j in range(2):
                    o, c0 = R(rb, 512 * j, 512 * j + 512), 1024 * h + 512 * j
                    mm.append((o, I, R("l%d" % y, c0, c0 + 512), True, False))
                    mm.append((o, ET, R("Ind", c0, c0 + 512, 1, (0, 64)), False, True))
                pe(mm)
                act(tile("vo", y, h), R(rb, 0, 1024), AF.Abs)
            if BSPLIT:
                for h in range(2):
                    pe(sums(R("ZB", 320 + 64 * h, 384 + 64 * h), [("Bp", "vb%d" % y, 1024 * h)]))
                act(F("Bsb"), R("ZB", 320, 448), AF.Copy)
            for h in range(2):
                q = [("Bn", "rq%d" % y, 1024 * h)] + ([] if (t, X) in DABS else [("Bp", "dq%d" % y, 1024 * h)])
                bs = [(R("idf", 0, 128), R(F("Bsb")[0], F("Bsb")[1] + 64 * h, F("Bsb")[1] + 64 * h + 64))]
                b = [("Bp", "vb%d" % y, 1024 * h)]
                pe(sums(R("SB", 64 * h, 64 * h + 64), q + ([] if BSPLIT else b), bs if BSPLIT else ()))
            for h in range(2):
                bs = [(R("idf", 0, 128), R(F("Bsb")[0], F("Bsb")[1] + 64 * h, F("Bsb")[1] + 64 * h + 64))]
                b = [("Bp", "vb%d" % y, 1024 * h)]
                pe(sums(R("CB", 64 * h, 64 * h + 64), ([] if BSPLIT else b) + [("Bn", "vc%d" % y, 1024 * h)], bs if BSPLIT else ()))
            act(F("Csb"), R("CB", 0, 128), AF.Copy)
            Z = R("ZB", 0, 64)
            zc = [(Z, R("blk2", 0, 128), every(F("Csb"), 0), False, False),
                  (Z, R("blk2", 0, 128), every(F("Csb"), 1), False, True)]
            if ASTAT:
                zc[0] = zc[0][:3] + (True, False)
                zc[1] = zc[1][:3] + (False, False)
                zc.append((Z, R("grp8", 0, 128, 1, (0, 8)), R(F("As2")[0], F("As2")[1], F("As2")[2], 1, (0, 8)), False, True))
            else:
                mm = []
                for k in range(32):
                    mm.append((Z, R("blkP", 0, 128), R("ra%d" % z, k, CH, 32), k == 0, False))
                    mm.append((Z, R("blkN", 0, 128), R("dp%d" % z, k, CH, 32), False, False))
                pe(mm)
            pe(zc)
            for h in range(2):
                pe(sums(R("SB", 128 + 64 * h, 192 + 64 * h), [("Bp", "vo%d" % y, 1024 * h)],
                        [(R(wn, W + 128, W + 256), R("one", 0, 64)), (R(wn, W + 256, W + 384), R("one", 0, 64))]))
            if t == 0:
                colA = "k37"
                cb = 0
            else:
                colA, cb = "af", t * 16 + 8
                if X == 0:
                    cn = R("MB", 192, 193)
                    pe([(cn, R("o16", 0, 128), R("eland", (sl - 2) * 80 + 64, (sl - 2) * 80 + 65), True, False),
                        (cn, R("o16", 0, 128), R("eland", (sl - 1) * 80 + 64, (sl - 1) * 80 + 65), False, True)])
                    vcopy(R("ai", t * 16, t * 16 + 1), cn)
                    vts(R("ai", t * 16 + 8, t * 16 + 9), R("ai", t * 16, t * 16 + 1), 31, OP.bitwise_and)
                    vts(R("af", t * 16, t * 16 + 1), R("ai", t * 16 + 8, t * 16 + 9), 32.0, OP.mult)
                    vts(R("af", t * 16 + 8, t * 16 + 10), R("k37", 0, 2), R("af", t * 16, t * 16 + 1), OP.add)
            for h in range(2):
                vts(every(J("LUi"), h), every(F("LU"), h), R(colA, cb + h, cb + h + 1), OP.add)
            vts(J("CHi"), J("LUi"), 5, OP.arith_shift_right, 2047, OP.bitwise_and)
            vts(F("CHp"), J("CHi"), 2048.0, OP.add)
            pe([(R("MB", 256, 320), I, E, True, False), (R("MB", 256, 320), NIDN, MR, False, True),
                (R("MB", 320, 384), I, E, True, False), (R("MB", 320, 384), I, MR, False, True)])
            ABE, WE2 = R("MB", 384, 448), R("CB", 384, 448)
            act(ABE, R("MB", 256, 320), AF.Abs)
            vts(J("h"), R("MB", 320, 384), 0.5, OP.mult, -0.25, OP.add)
            vtt(F("w"), ABE, J("h"), OP.subtract)
            D, O, C = R("SB", 0, 128), R("SB", 128, 256), R("CB", 0, 128)
            vtt(D, Qv(t, X), D, OP.min)
            FAIL = R("ZB", 64, 128)
            vts(FAIL, Z, 0.0, OP.is_gt)
            for h in range(2):
                vtt(every(F("PF"), h), every(L6(t - 2, X), h), FAIL, OP.mult)
            vtt(C, F("PF"), C, OP.min)
            vtt(F("r3"), L, D, OP.max)
            vtt(F("r2"), F("r3"), C, OP.max)
            vtt(O, F("CHp"), O, OP.min)
            vtt(J("r1"), F("r2"), O, OP.max)
            NEW = Ln(t + 1, X)
            vts(NEW, J("r1"), 2047, OP.bitwise_and)
            last = t == NV - 1
            if not last:
                vcopy(Lu(t + 1, X, None), NEW)
                if t + 1 <= NV - 3:
                    vts(L6(t + 1, X), NEW, 6144.0, OP.add)
            q1, q2 = R("CB", 128, 256), R("CB", 256, 384)
            vtt(q1, NEW, L, OP.not_equal)
            vtt(q2, F("LQ"), q1, OP.mult)
            if not last:
                vtt(Qv(t + 1, X), Qv(t, X), q2, OP.add)
                vts(Qu(t + 1, X, None), Qv(t + 1, X), -4096.0, OP.add)
            EM = R("emsg", sl * 80, sl * 80 + 64)
            vtt(WE2, F("w"), FAIL, OP.mult)
            vtt(EM, J("h"), WE2, OP.add)
            c8 = F("cnt")
            if not last:
                act(F("junk"), FAIL, AF.Copy, acc_out=R(c8[0], c8[1], c8[1] + 1))
                act(R("emsg", sl * 80 + 64, sl * 80 + 65), R(c8[0], c8[1], c8[1] + 1), AF.Copy)
            send(rank - HOP if not last else rank - 1, R("eland", sl * 80, sl * 80 + 72), R("emsg", sl * 80, sl * 80 + 72), "e%d" % sl)
            if last:
                q3 = R("tf", z * NF + FT["r2"][0], z * NF + FT["r2"][0] + 128)
                vtt(q3, Qv(t, X), q2, OP.add)
                vcopy(R("finLQ", 256 * X, 256 * X + 128), NEW)
                vts(R("finLQ", 256 * X + 128, 256 * X + 256), q3, -4096.0, OP.add)
                send(rank - 1, R("fLQ", 256 * X, 256 * X + 256), R("finLQ", 256 * X, 256 * X + 256), "fb" if X == 0 else "fc")
                if X == 0:
                    vcopy(R("finPS", 0, 256), R("Lnum", 3 * 256, 4 * 256))
                    vcopy(R("finPS", 256, 512), R("Lnum", 4 * 256, 5 * 256))
                    send(rank - 1, R("fPS", 0, 512), R("finPS", 0, 512), "fa")
                    store("Y", "yp", 0, 256, R("fPS", 0, 256), "st0")
                    store("Y", "ys", 0, 256, R("fPS", 256, 512), "st1")
                store("Y", "yl", 128 * X, 128 * X + 128, R("fLQ", 256 * X, 256 * X + 128), "st%d" % (2 + 4 * X))
                store("S", "yq", 128 * X, 128 * X + 128, R("fLQ", 256 * X + 128, 256 * X + 256), "st%d" % (3 + 4 * X))
                store("Y", "ye", 64 * X, 64 * X + 64, R("eland", sl * 80, sl * 80 + 64), "st%d" % (4 + 4 * X))

    n = len(ops)
    succ = [[] for _ in range(n)]
    for k in range(n):
        for d in ops[k]["dep"]:
            succ[d].append(k)
    prio = [0.0] * n
    for k in range(n - 1, -1, -1):
        prio[k] = ops[k]["lat"] + max([prio[s] + 0.08 for s in succ[k]] + [0.0])
    left = [len(ops[k]["dep"]) for k in range(n)]
    rdy = [0.0] * n
    free = {"V": 0.0, "S": 0.0, "P": 0.0, "G": 0.0, "Y": 0.0}
    pool = {"V": [], "S": [], "P": [], "G": [], "Y": [], "N": []}
    for k in range(n):
        if left[k] == 0:
            pool[ops[k]["eng"]].append(k)
    order = []
    while len(order) < n:
        best = None
        for e in pool:
            if pool[e]:
                m = min(rdy[k] for k in pool[e])
                s = m if e == "N" else max(free[e], m)
                if best is None or s < best[0]:
                    best = (s, e)
        s, e = best
        k = max([k for k in pool[e] if rdy[k] <= s + 1e-9], key=lambda q: (prio[q] + ops[q]["boost"], -q))
        pool[e].remove(k)
        order.append(k)
        if e != "N":
            free[e] = s + ops[k]["occ"]
        fin = s + ops[k]["lat"]
        for q in succ[k]:
            left[q] -= 1
            rdy[q] = max(rdy[q], fin + 0.08)
            if left[q] == 0:
                pool[ops[q]["eng"]].append(q)

    known = {e: {} for e in ENG}
    count = {"sV": 0, "sS": 0, "sP": 0, "sG": 0}
    event = [None] * n
    snap = [None] * n
    total = {}
    pos = {k: i for i, k in enumerate(order)}
    for k in order:
        o = ops[k]
        e = o["eng"]
        if e == "N":
            event[k] = (o["sem"], o["inc"])
            total[o["sem"]] = o["inc"]
            snap[k] = {}
            continue
        kn = known[e]
        for d in sorted(o["dep"], key=lambda q: -pos[q]):
            if event[d] is None:
                continue
            sm, v = event[d]
            if kn.get(sm, 0) >= v:
                continue
            ENG[e].wait_ge(T.sem[sm], v)
            kn[sm] = v
            for a, b in snap[d].items():
                if kn.get(a, 0) < b:
                    kn[a] = b
        ins = o["emit"](ENG[e])
        if o["sem"] is None:
            sm = ESEM[e]
            for x in ins:
                x.then_inc(T.sem[sm], 1)
            count[sm] += len(ins)
            event[k] = (sm, count[sm])
            total[sm] = count[sm]
        elif o["inc"]:
            for x in ins:
                x.then_inc(T.sem[o["sem"]], o["inc"])
            event[k] = (o["sem"], o["inc"])
            total[o["sem"]] = o["inc"]
        snap[k] = dict(kn)
    total["lsem"] = nsent[0]
    for sm in total:
        if known["G"].get(sm, 0) < total[sm]:
            g.wait_ge(T.sem[sm], total[sm])
